import numpy as np
import ml_dtypes

BF16 = ml_dtypes.bfloat16


def bf(x):
    return np.asarray(x, np.float32).astype(BF16)


def f32(x):
    return np.asarray(x, np.float32)


def f64(x):
    return np.asarray(x).astype(np.float64)


def striped(idx):
    return np.tile(idx.reshape(-1, 16).T, (8, 1))


def rows(idx, k):
    return np.tile(idx, (k, 1))


def look(tab, idx):
    return np.take_along_axis(f64(tab), rows(idx, len(tab)), axis=1)


K, S, V, N, M = 128, 2048, 1024, 1024, 128


def setup_inputs():
    return {"tab": f32(np.random.standard_normal((K, S))), "y": f32(np.random.standard_normal((K, V))), "w": bf(np.random.standard_normal((K, M)) / np.sqrt(K)), "b": f32(0.5 * np.random.standard_normal((M, 1))), "offs": striped(np.random.permutation(S)[:N])}


def reference(tab, y, w, b, offs):
    idx = offs[:16].T.reshape(-1)
    t = look(tab, idx)
    x = t**2 * f64(y)
    y = f64(w).T @ x
    return np.maximum(y + f64(b), 0.0)

@@ -1,0 +1,49 @@
+import concourse.mybir as mybir
+
+F32, BF16, U16 = mybir.dt.float32, mybir.dt.bfloat16, mybir.dt.uint16
+SQUARE = mybir.ActivationFunctionType.Square
+ADD, MAX, MULT = mybir.AluOpType.add, mybir.AluOpType.max, mybir.AluOpType.mult
+
+P = 128
+TABLE_COLUMNS = 2048
+N = 1024
+LANES = 16
+PIECE = 256
+FLOPS = 2 * P * P * N
+
+
+def tile_lookup_gate_sq_relu_kernel(tc, tab, y, w, b, offs, out):
+    nc = tc.nc
+    with (
+        tc.tile_pool(name="held", bufs=1) as held,
+        tc.tile_pool(name="ring", bufs=2) as ring,
+        tc.psum_pool(name="psum", bufs=2) as psum,
+    ):
+        offsets = held.tile([P, N // LANES], U16, name="offsets")
+        table = held.tile([P, TABLE_COLUMNS], F32, name="table")
+        stream = held.tile([P, N], F32, name="stream")
+        weights = held.tile([P, P], BF16, name="weights")
+        bias = held.tile([P, 1], F32, name="bias")
+
+        nc.sync.dma_start(offsets[:], offs)
+        nc.sync.dma_start(table[:], tab)
+        nc.sync.dma_start(stream[:], y)
+        nc.scalar.dma_start(weights[:], w)
+        nc.scalar.dma_start(bias[:], b)
+
+        for first in range(0, N, PIECE):
+            piece = slice(first, first + PIECE)
+            listed = offsets[:, first // LANES : (first + PIECE) // LANES]
+
+            squared = ring.tile([P, PIECE], F32, name="squared")
+            nc.scalar.activation(squared[:], table[:].indirect(listed), SQUARE)
+
+            gated = ring.tile([P, PIECE], BF16, name="gated")
+            nc.vector.tensor_tensor(gated[:], squared[:], stream[:, piece], MULT)
+
+            product = psum.tile([P, PIECE], F32, name="product")
+            nc.tensor.matmul(product[:], weights[:], gated[:], start=True, stop=True)
+
+            layer = ring.tile([P, PIECE], F32, name="layer")
+            nc.vector.tensor_scalar(layer[:], product[:], bias[:], 0.0, op0=ADD, op1=MAX)
+            nc.sync.dma_start(out[:, piece], layer[:])

@@ -16,8 +16,8 @@ def tile_lookup_gate_sq_relu_kernel(tc, tab, y, w, b, offs, out):
     nc = tc.nc
     with (
         tc.tile_pool(name="held", bufs=1) as held,
-        tc.tile_pool(name="ring", bufs=2) as ring,
-        tc.psum_pool(name="psum", bufs=2) as psum,
+        tc.tile_pool(name="ring", bufs=N // PIECE) as ring,
+        tc.psum_pool(name="psum", bufs=N // PIECE) as psum,
     ):
         offsets = held.tile([P, N // LANES], U16, name="offsets")
         table = held.tile([P, TABLE_COLUMNS], F32, name="table")
@@ -28,8 +28,13 @@ def tile_lookup_gate_sq_relu_kernel(tc, tab, y, w, b, offs, out):
         nc.sync.dma_start(offsets[:], offs)
         nc.sync.dma_start(table[:], tab)
         nc.sync.dma_start(stream[:], y)
-        nc.scalar.dma_start(weights[:], w)
         nc.scalar.dma_start(bias[:], b)
+        nc.scalar.dma_start(weights[:], w)
+
+        zeros = held.tile([P, 1], F32, name="zeros")
+        warmed = held.tile([P, 1], F32, name="warmed")
+        nc.vector.memset(zeros[:], 0.0)
+        nc.scalar.activation(warmed[:], zeros[:], SQUARE)
 
         for first in range(0, N, PIECE):
             piece = slice(first, first + PIECE)

@@ -2,13 +2,14 @@ import concourse.mybir as mybir
 
 F32, BF16, U16 = mybir.dt.float32, mybir.dt.bfloat16, mybir.dt.uint16
 SQUARE = mybir.ActivationFunctionType.Square
+RELU = mybir.ActivationFunctionType.Relu
 ADD, MAX, MULT = mybir.AluOpType.add, mybir.AluOpType.max, mybir.AluOpType.mult
 
 P = 128
 TABLE_COLUMNS = 2048
 N = 1024
 LANES = 16
-PIECE = 256
+PIECES = (256, 256, 256, 128, 128)
 FLOPS = 2 * P * P * N
 
 
@@ -16,8 +17,8 @@ def tile_lookup_gate_sq_relu_kernel(tc, tab, y, w, b, offs, out):
     nc = tc.nc
     with (
         tc.tile_pool(name="held", bufs=1) as held,
-        tc.tile_pool(name="ring", bufs=N // PIECE) as ring,
-        tc.psum_pool(name="psum", bufs=N // PIECE) as psum,
+        tc.tile_pool(name="pieces", bufs=1) as pieces,
+        tc.psum_pool(name="psum", bufs=1) as psum,
     ):
         offsets = held.tile([P, N // LANES], U16, name="offsets")
         table = held.tile([P, TABLE_COLUMNS], F32, name="table")
@@ -27,7 +28,8 @@ def tile_lookup_gate_sq_relu_kernel(tc, tab, y, w, b, offs, out):
 
         nc.sync.dma_start(offsets[:], offs)
         nc.sync.dma_start(table[:], tab)
-        nc.sync.dma_start(stream[:], y)
+        for half in (slice(0, N // 2), slice(N // 2, N)):
+            nc.sync.dma_start(stream[:, half], y[:, half])
         nc.scalar.dma_start(bias[:], b)
         nc.scalar.dma_start(weights[:], w)
 
@@ -36,19 +38,26 @@ def tile_lookup_gate_sq_relu_kernel(tc, tab, y, w, b, offs, out):
         nc.vector.memset(zeros[:], 0.0)
         nc.scalar.activation(warmed[:], zeros[:], SQUARE)
 
-        for first in range(0, N, PIECE):
-            piece = slice(first, first + PIECE)
-            listed = offsets[:, first // LANES : (first + PIECE) // LANES]
-
-            squared = ring.tile([P, PIECE], F32, name="squared")
+        products = []
+        first = 0
+        for k, size in enumerate(PIECES):
+            piece = slice(first, first + size)
+            listed = offsets[:, first // LANES : (first + size) // LANES]
+            squared = pieces.tile([P, size], F32, name=f"squared{k}")
             nc.scalar.activation(squared[:], table[:].indirect(listed), SQUARE)
 
-            gated = ring.tile([P, PIECE], BF16, name="gated")
+            gated = pieces.tile([P, size], BF16, name=f"gated{k}")
             nc.vector.tensor_tensor(gated[:], squared[:], stream[:, piece], MULT)
 
-            product = psum.tile([P, PIECE], F32, name="product")
+            product = psum.tile([P, size], F32, name=f"product{k}")
             nc.tensor.matmul(product[:], weights[:], gated[:], start=True, stop=True)
+            products.append((piece, product))
+            first += size
 
-            layer = ring.tile([P, PIECE], F32, name="layer")
-            nc.vector.tensor_scalar(layer[:], product[:], bias[:], 0.0, op0=ADD, op1=MAX)
+        for k, (piece, product) in enumerate(products):
+            layer = pieces.tile([P, PIECES[k]], F32, name=f"layer{k}")
+            if k % 2 == 0:
+                nc.vector.tensor_scalar(layer[:], product[:], bias[:], 0.0, op0=ADD, op1=MAX)
+            else:
+                nc.scalar.activation(layer[:], product[:], RELU, bias=bias[:])
             nc.sync.dma_start(out[:, piece], layer[:])

@@ -27,11 +27,12 @@ def tile_lookup_gate_sq_relu_kernel(tc, tab, y, w, b, offs, out):
         bias = held.tile([P, 1], F32, name="bias")
 
         nc.sync.dma_start(offsets[:], offs)
-        nc.sync.dma_start(table[:], tab)
-        for half in (slice(0, N // 2), slice(N // 2, N)):
-            nc.sync.dma_start(stream[:, half], y[:, half])
-        nc.scalar.dma_start(bias[:], b)
+        left, right = slice(0, TABLE_COLUMNS // 2), slice(TABLE_COLUMNS // 2, TABLE_COLUMNS)
+        nc.sync.dma_start(table[:, left], tab[:, left])
+        nc.scalar.dma_start(table[:, right], tab[:, right])
+        nc.sync.dma_start(stream[:], y)
         nc.scalar.dma_start(weights[:], w)
+        nc.scalar.dma_start(bias[:], b)
 
         zeros = held.tile([P, 1], F32, name="zeros")
         warmed = held.tile([P, 1], F32, name="warmed")

import concourse.mybir as mybir

F32, BF16, U16 = mybir.dt.float32, mybir.dt.bfloat16, mybir.dt.uint16
SQUARE = mybir.ActivationFunctionType.Square
RELU = mybir.ActivationFunctionType.Relu
ADD, MAX, MULT = mybir.AluOpType.add, mybir.AluOpType.max, mybir.AluOpType.mult

P = 128
TABLE_COLUMNS = 2048
N = 1024
LANES = 16
PIECES = (256, 256, 256, 128, 128)
FLOPS = 2 * P * P * N


def tile_lookup_gate_sq_relu_kernel(tc, tab, y, w, b, offs, out):
    nc = tc.nc
    with (
        tc.tile_pool(name="held", bufs=1) as held,
        tc.tile_pool(name="pieces", bufs=1) as pieces,
        tc.psum_pool(name="psum", bufs=1) as psum,
    ):
        offsets = held.tile([P, N // LANES], U16, name="offsets")
        table = held.tile([P, TABLE_COLUMNS], F32, name="table")
        stream = held.tile([P, N], F32, name="stream")
        weights = held.tile([P, P], BF16, name="weights")
        bias = held.tile([P, 1], F32, name="bias")

        nc.sync.dma_start(offsets[:], offs)
        left, right = slice(0, TABLE_COLUMNS // 2), slice(TABLE_COLUMNS // 2, TABLE_COLUMNS)
        nc.sync.dma_start(table[:, left], tab[:, left])
        nc.scalar.dma_start(table[:, right], tab[:, right])
        nc.sync.dma_start(stream[:], y)
        nc.scalar.dma_start(weights[:], w)
        nc.scalar.dma_start(bias[:], b)

        zeros = held.tile([P, 1], F32, name="zeros")
        warmed = held.tile([P, 1], F32, name="warmed")
        nc.vector.memset(zeros[:], 0.0)
        nc.scalar.activation(warmed[:], zeros[:], SQUARE)

        products = []
        first = 0
        for k, size in enumerate(PIECES):
            piece = slice(first, first + size)
            listed = offsets[:, first // LANES : (first + size) // LANES]
            squared = pieces.tile([P, size], F32, name=f"squared{k}")
            nc.scalar.activation(squared[:], table[:].indirect(listed), SQUARE)

            gated = pieces.tile([P, size], BF16, name=f"gated{k}")
            nc.vector.tensor_tensor(gated[:], squared[:], stream[:, piece], MULT)

            product = psum.tile([P, size], F32, name=f"product{k}")
            nc.tensor.matmul(product[:], weights[:], gated[:], start=True, stop=True)
            products.append((piece, product))
            first += size

        for k, (piece, product) in enumerate(products):
            layer = pieces.tile([P, PIECES[k]], F32, name=f"layer{k}")
            if k % 2 == 0:
                nc.vector.tensor_scalar(layer[:], product[:], bias[:], 0.0, op0=ADD, op1=MAX)
            else:
                nc.scalar.activation(layer[:], product[:], RELU, bias=bias[:])
            nc.sync.dma_start(out[:, piece], layer[:])
